import numpy as np, ml_dtypes
CORES = [17,81,89,18,82,90]
N = 6
F = 512
GROUPS = [[0,1,2],[3,4,5]]
def setup_inputs(rng):
    return {"x": rng.standard_normal((N, 128, F), dtype=np.float32).astype(ml_dtypes.bfloat16), "w": (rng.standard_normal((N, 128, 128), dtype=np.float32) / 11).astype(ml_dtypes.bfloat16)}
def setup_inputs_big(rng):
    d = setup_inputs(rng)
    for k in ("x", "w"): d[k] = (d[k].astype(np.float32) * 1024.0).astype(d[k].dtype)
    return d
def setup_inputs_small(rng):
    d = setup_inputs(rng)
    for k in ("x", "w"): d[k] = (d[k].astype(np.float32) * (1 / 1024.0)).astype(d[k].dtype)
    return d
def setup_inputs_apart(rng):
    d = setup_inputs(rng)
    f = (10.0 ** rng.permutation(np.linspace(-1.5, 1.5, N))).astype(np.float32).reshape(N, 1, 1)
    for k in ("x", "w"): d[k] = (d[k].astype(np.float32) * f).astype(d[k].dtype)
    return d
def reference(x, w):
    X, W = x.astype(np.float64), w.astype(np.float64)
    s = sum(W[g[0]].T @ np.maximum(sum(X[j] for j in g), 0.0) for g in GROUPS).astype(ml_dtypes.bfloat16)
    return {"y": np.broadcast_to(s, (N,) + s.shape)}

@@ -1,0 +1,239 @@
+from concourse.bass import DstId, RemoteDMATransfer
+from concourse.mybir import AluOpType
+
+F = 512
+H = 256
+M = 128
+
+SCRATCH = {
+    "xs": ("sbuf", [128, F], "bfloat16"),
+    "wcat": ("sbuf", [128, 2 * M], "bfloat16"),
+    "hl": ("sbuf", [128, H], "bfloat16"),
+    "land0": ("sbuf", [128, H], "bfloat16"),
+    "land1": ("sbuf", [128, H], "bfloat16"),
+    "land2": ("sbuf", [128, H], "bfloat16"),
+    "land3": ("sbuf", [128, H], "bfloat16"),
+    "land4": ("sbuf", [128, H], "bfloat16"),
+    "land5": ("sbuf", [128, H], "bfloat16"),
+    "zero": ("sbuf", [128, H], "bfloat16"),
+    "t0": ("sbuf", [128, H], "bfloat16"),
+    "t1": ("sbuf", [128, H], "bfloat16"),
+    "yh": ("sbuf", [128, H], "bfloat16"),
+    "yo": ("sbuf", [128, H], "bfloat16"),
+    "pa0": ("psum", [128, 512], "float32"),
+    "pb0": ("psum", [128, 512], "float32"),
+    "pa1": ("psum", [128, 512], "float32"),
+    "pb1": ("psum", [128, 512], "float32"),
+    "py": ("psum", [128, 512], "float32"),
+}
+SEMAPHORES = ["ldx", "ldw", "zs", "ah", "aw", "a0", "a1", "a2", "a3", "a4", "a5",
+              "va0", "va1", "vb0", "vb1", "vt0", "vt1", "pm", "vy", "ay", "st1", "st2", "ls"]
+
+
+def _bits(mask):
+    return [i for i in range(mask.bit_length()) if (mask >> i) & 1]
+
+
+def _mk(bits):
+    m = 0
+    for b in bits:
+        m |= 1 << b
+    return m
+
+
+def _plan(T, topo):
+    C = list(T.cores)
+    G = T.tables["GROUPS"]
+    N = len(C)
+    chip_of = [topo.chip(c) for c in C]
+    chips = sorted(set(chip_of))
+    on_chip = {ch: [r for r in range(N) if chip_of[r] == ch] for ch in chips}
+    half = {}
+    for ch in chips:
+        for i, r in enumerate(on_chip[ch]):
+            half[r] = i
+    every = range(topo.CHIPS * topo.CORES_PER_CHIP)
+    free = {ch: [c for c in every if topo.chip(c) == ch and c not in C] for ch in chips}
+
+    def pick(src, dsts):
+        ch = topo.chip(src)
+        ok = [c for c in free[ch] if all(topo.may_write(c, d) for d in dsts)]
+        ok.sort(key=lambda c: (topo.die(c) == topo.die(src), c))
+        free[ch].remove(ok[0])
+        return ok[0]
+
+    calls, expect, cls = {}, {}, {}
+
+    def add(core, waits, trs):
+        calls.setdefault(core, []).append((waits, trs))
+        for (_sn, _sc, dl, sem, mask) in trs:
+            for (dc, _dn, _dcs) in dl:
+                expect[(dc, sem)] = expect.get((dc, sem), 0) + len(_bits(mask))
+
+    def common(src, dsts):
+        m = topo.mask(src, dsts[0])
+        for d in dsts[1:]:
+            m &= topo.mask(src, d)
+        return m
+
+    route = {}
+    for j in range(N):
+        near, direct, blocked = [], {}, {}
+        for r in range(N):
+            if r == j:
+                cls[(r, j)] = 0
+            elif chip_of[r] == chip_of[j]:
+                near.append(r)
+                cls[(r, j)] = 1
+            elif topo.may_write(C[j], C[r]):
+                direct.setdefault(half[r], []).append(r)
+                cls[(r, j)] = 1
+            else:
+                blocked.setdefault(half[r], []).append(r)
+                cls[(r, j)] = 2
+        relay = {h: pick(C[j], [C[r] for r in blocked[h]]) for h in sorted(blocked)}
+        route[j] = (near, direct, blocked, relay)
+    owners = [m[0] for m in G]
+    home = chip_of[owners[0]]
+    whelp = {ch: pick(C[owners[0]], [C[r] for r in on_chip[ch]]) for ch in chips if ch != home}
+
+    for j in range(N):
+        src = C[j]
+        near, direct, blocked, relay = route[j]
+        if j in owners:
+            q = owners.index(j)
+            wc = (q * M, (q + 1) * M)
+            dl = [whelp[ch] for ch in sorted(whelp)] + [C[r] for r in on_chip[home] if r != j]
+            add(src, [("ldw", 16)], [("wcat", wc, [(d, "wcat", wc) for d in dl], "aw", common(src, dl))])
+        if blocked:
+            hs = sorted(blocked)
+            trs = []
+            for i, h in enumerate(hs):
+                b = _bits(topo.mask(src, relay[h]))
+                n = len(b) // len(hs)
+                trs.append(("xs", (h * H, (h + 1) * H), [(relay[h], "hl", None)], "ah", _mk(b[i * n:(i + 1) * n])))
+            add(src, [("ldx", 16)], trs)
+            for h in hs:
+                ds = [C[r] for r in blocked[h]]
+                add(relay[h], [("ah", None)],
+                    [("hl", None, [(d, "land%d" % j, None) for d in ds], "a%d" % j, common(relay[h], ds))])
+        trs = []
+        used = []
+        hs = sorted(direct)
+        for i, h in enumerate(hs):
+            ds = [C[r] for r in direct[h]]
+            b = _bits(common(src, ds))
+            n = len(b) // len(hs)
+            used += b
+            trs.append(("xs", (h * H, (h + 1) * H), [(d, "land%d" % j, None) for d in ds], "a%d" % j,
+                        _mk(b[i * n:(i + 1) * n])))
+        for r in near:
+            b = [e for e in _bits(topo.mask(src, C[r])) if e not in used]
+            h = half[r]
+            trs.append(("xs", (h * H, (h + 1) * H), [(C[r], "land%d" % j, None)], "a%d" % j, _mk(b)))
+        add(src, [("ldx", 16)], trs)
+    for ch in sorted(whelp):
+        ds = [C[r] for r in on_chip[ch]]
+        add(whelp[ch], [("aw", None)], [("wcat", None, [(d, "wcat", None) for d in ds], "aw", common(whelp[ch], ds))])
+    for j in range(N):
+        for r in route[j][0]:
+            add(C[j], [("vy", 1)], [("yh", None, [(C[r], "yo", None)], "ay", topo.mask(C[j], C[r]))])
+    return {"calls": calls, "expect": expect, "cls": cls, "half": half, "owners": owners, "groups": G}
+
+
+def rank_program(g, core, T, topo):
+    P = _plan(T, topo)
+    calls, expect = P["calls"], P["expect"]
+    if core not in calls:
+        return
+    S = T.sem
+    rank = T.rank_of(core)
+
+    def ap(name, cols):
+        return T[name][:] if cols is None else T[name][:, cols[0]:cols[1]]
+
+    def issue():
+        sent = 0
+        for waits, trs in calls[core]:
+            for s, v in waits:
+                g.wait_ge(S[s], expect[(core, s)] if v is None else v)
+            lst = []
+            for (sn, sc, dl, sem, mask) in trs:
+                ids = []
+                for (dc, _dn, _dcs) in dl:
+                    rid, pid, _se = topo.addr(dc)
+                    ids.append(DstId(rid=rid, pnc=pid))
+                lst.append(RemoteDMATransfer(dst_ids=ids, dma_engine_mask=mask, remote_sem=S[sem],
+                                             srcs=[ap(sn, sc)], dsts=[ap(dn, dcs) for (_dc, dn, dcs) in dl], alu_op=0))
+                sent += len(_bits(mask))
+            g.remote_dma_fused(lst, local_sem=S.ls)
+        return sent
+
+    if rank is None:
+        g.wait_ge(S.ls, issue())
+        return
+
+    h = P["half"][rank]
+    own = (h * H, (h + 1) * H)
+    oth = ((1 - h) * H, (2 - h) * H)
+    V, PE = g.vector, g.tensor
+
+    if rank in P["owners"]:
+        q = P["owners"].index(rank)
+        g.scalar.dma_start(T.wcat[:, q * M:(q + 1) * M], T.w[:]).then_inc(S.ldw, 16)
+    g.sync.dma_start(T.xs[:], T.x[:]).then_inc(S.ldx, 16)
+    V.memset(T.zero[:], 0.0).then_inc(S.zs, 1)
+
+    def piece(j):
+        if j == rank:
+            return ap("xs", own), ("ldx", 16)
+        return T["land%d" % j][:], ("a%d" % j, expect[(core, "a%d" % j)])
+
+    cls = P["cls"]
+    order = {}
+    for q, mem in enumerate(P["groups"]):
+        order[q] = sorted(mem, key=lambda j: cls[(rank, j)])
+    gs = sorted(order, key=lambda q: cls[(rank, order[q][-1])])
+    ops = []
+    for q in gs:
+        ops.append((cls[(rank, order[q][1])], "A", q))
+        ops.append((cls[(rank, order[q][2])], "B", q))
+        ops.append((cls[(rank, order[q][2])], "T", q))
+    ops.sort(key=lambda o: o[0])
+    for (_k, kind, q) in ops:
+        pa, pb = T["pa%d" % q][:, 0:H], T["pb%d" % q][:, 0:H]
+        if kind == "A":
+            (a0, w0), (a1, w1) = piece(order[q][0]), piece(order[q][1])
+            V.wait_ge(S[w0[0]], w0[1])
+            V.wait_ge(S[w1[0]], w1[1])
+            V.tensor_tensor(out=pa, in0=a0, in1=a1, op=AluOpType.add).then_inc(S["va%d" % q], 1)
+        elif kind == "B":
+            a2, w2 = piece(order[q][2])
+            V.wait_ge(S[w2[0]], w2[1])
+            V.wait_ge(S["va%d" % q], 1)
+            V.tensor_tensor(out=pb, in0=pa, in1=a2, op=AluOpType.add).then_inc(S["vb%d" % q], 1)
+        else:
+            V.wait_ge(S.zs, 1)
+            V.wait_ge(S["vb%d" % q], 1)
+            V.tensor_tensor(out=T["t%d" % q][:], in0=pb, in1=T.zero[:], op=AluOpType.max).then_inc(S["vt%d" % q], 1)
+
+    if rank in P["owners"]:
+        PE.wait_ge(S.ldw, 16)
+    PE.wait_ge(S.aw, expect[(core, "aw")])
+    for i, q in enumerate(gs):
+        PE.wait_ge(S["vt%d" % q], 1)
+        mm = PE.matmul(out=T.py[:, 0:H], lhsT=T.wcat[:, q * M:(q + 1) * M], rhs=T["t%d" % q][:],
+                       start=(i == 0), stop=(i == len(gs) - 1))
+        if i == len(gs) - 1:
+            mm.then_inc(S.pm, 1)
+    V.wait_ge(S.pm, 1)
+    V.tensor_copy(out=T.yh[:], in_=T.py[:, 0:H]).then_inc(S.vy, 1)
+
+    g.sync.wait_ge(S.vy, 1)
+    g.sync.dma_start(T.y[:, own[0]:own[1]], T.yh[:]).then_inc(S.st1, 16)
+    g.scalar.wait_ge(S.ay, expect[(core, "ay")])
+    g.scalar.dma_start(T.y[:, oth[0]:oth[1]], T.yo[:]).then_inc(S.st2, 16)
+
+    g.wait_ge(S.ls, issue())
+    g.wait_ge(S.st1, 16)
+    g.wait_ge(S.st2, 16)

@@ -1,33 +1,41 @@
 from concourse.bass import DstId, RemoteDMATransfer
-from concourse.mybir import AluOpType
+from concourse.mybir import AluOpType, ActivationFunctionType
 
 F = 512
 H = 256
 M = 128
+NCH = 2
+CW = H // NCH
 
 SCRATCH = {
-    "xs": ("sbuf", [128, F], "bfloat16"),
+    "xd": ("dram", [2, 128, H], "bfloat16"),
+    "hd": ("dram", [2, 128, H], "bfloat16"),
+    "wd": ("dram", [128, M], "bfloat16"),
+    "wh": ("dram", [2, 128, M], "bfloat16"),
+    "xo": ("sbuf", [128, H], "bfloat16"),
     "wcat": ("sbuf", [128, 2 * M], "bfloat16"),
-    "hl": ("sbuf", [128, H], "bfloat16"),
     "land0": ("sbuf", [128, H], "bfloat16"),
     "land1": ("sbuf", [128, H], "bfloat16"),
     "land2": ("sbuf", [128, H], "bfloat16"),
     "land3": ("sbuf", [128, H], "bfloat16"),
     "land4": ("sbuf", [128, H], "bfloat16"),
     "land5": ("sbuf", [128, H], "bfloat16"),
-    "zero": ("sbuf", [128, H], "bfloat16"),
+    "ones": ("sbuf", [128, 128], "bfloat16"),
+    "ident": ("sbuf", [128, 128], "bfloat16"),
     "t0": ("sbuf", [128, H], "bfloat16"),
     "t1": ("sbuf", [128, H], "bfloat16"),
     "yh": ("sbuf", [128, H], "bfloat16"),
     "yo": ("sbuf", [128, H], "bfloat16"),
-    "pa0": ("psum", [128, 512], "float32"),
-    "pb0": ("psum", [128, 512], "float32"),
-    "pa1": ("psum", [128, 512], "float32"),
-    "pb1": ("psum", [128, 512], "float32"),
-    "py": ("psum", [128, 512], "float32"),
+    "s00": ("psum", [128, 512], "float32"),
+    "s01": ("psum", [128, 512], "float32"),
+    "s10": ("psum", [128, 512], "float32"),
+    "s11": ("psum", [128, 512], "float32"),
+    "py0": ("psum", [128, 512], "float32"),
+    "py1": ("psum", [128, 512], "float32"),
 }
-SEMAPHORES = ["ldx", "ldw", "zs", "ah", "aw", "a0", "a1", "a2", "a3", "a4", "a5",
-              "va0", "va1", "vb0", "vb1", "vt0", "vt1", "pm", "vy", "ay", "st1", "st2", "ls"]
+SEMAPHORES = ["ldx", "ldw", "ldo", "ldc", "zs", "idn", "ah", "aw", "a0", "a1", "a2", "a3", "a4", "a5",
+              "ps00", "ps01", "ps10", "ps11", "vs0", "vs1", "vt00", "vt01", "vt10", "vt11", "pm0", "pm1",
+              "vy0", "vy1", "ay", "st1", "st2", "ls"]
 
 
 def _bits(mask):
@@ -53,16 +61,25 @@ def _plan(T, topo):
         for i, r in enumerate(on_chip[ch]):
             half[r] = i
     every = range(topo.CHIPS * topo.CORES_PER_CHIP)
-    free = {ch: [c for c in every if topo.chip(c) == ch and c not in C] for ch in chips}
+    spare = [c for c in every if c not in C and
+             (topo.chip(c) in chips or any(topo.mates(topo.chip(c), ch) for ch in chips))]
 
-    def pick(src, dsts):
-        ch = topo.chip(src)
-        ok = [c for c in free[ch] if all(topo.may_write(c, d) for d in dsts)]
-        ok.sort(key=lambda c: (topo.die(c) == topo.die(src), c))
-        free[ch].remove(ok[0])
-        return ok[0]
+    def pick(src, dsts, dst_first=False, reuse=()):
+        def ok(c):
+            return topo.may_write(src, c) and all(topo.may_write(c, d) for d in dsts)
 
-    calls, expect, cls = {}, {}, {}
+        def key(c):
+            if topo.chip(c) == topo.chip(src):
+                return (1 if dst_first else 0, topo.die(c) == topo.die(src), c)
+            if topo.chip(c) == topo.chip(dsts[0]):
+                return (0 if dst_first else 1, topo.die(c) != topo.die(dsts[0]), c)
+            return (2, topo.die(c) == topo.die(src), c)
+        c = sorted([c for c in list(spare) + list(reuse) if ok(c)], key=key)[0]
+        if c in spare:
+            spare.remove(c)
+        return c
+
+    calls, expect = {}, {}
 
     def add(core, waits, trs):
         calls.setdefault(core, []).append((waits, trs))
@@ -76,69 +93,120 @@ def _plan(T, topo):
             m &= topo.mask(src, d)
         return m
 
-    route = {}
-    for j in range(N):
-        near, direct, blocked = [], {}, {}
-        for r in range(N):
-            if r == j:
-                cls[(r, j)] = 0
-            elif chip_of[r] == chip_of[j]:
-                near.append(r)
-                cls[(r, j)] = 1
-            elif topo.may_write(C[j], C[r]):
-                direct.setdefault(half[r], []).append(r)
-                cls[(r, j)] = 1
-            else:
-                blocked.setdefault(half[r], []).append(r)
-                cls[(r, j)] = 2
-        relay = {h: pick(C[j], [C[r] for r in blocked[h]]) for h in sorted(blocked)}
-        route[j] = (near, direct, blocked, relay)
+    reach = {j: [d for d in chips if d != chip_of[j] and all(topo.may_write(C[j], C[r]) for r in on_chip[d])]
+             for j in range(N)}
+    direct = {}
+    for j in sorted(range(N), key=lambda j: (len(reach[j]), j)):
+        if not reach[j]:
+            direct[j] = None
+            continue
+        taken = [direct.get(p) for p in on_chip[chip_of[j]] if p != j]
+        direct[j] = sorted(reach[j], key=lambda d: (d in taken, not topo.mates(chip_of[j], d), d))[0]
+
     owners = [m[0] for m in G]
     home = chip_of[owners[0]]
-    whelp = {ch: pick(C[owners[0]], [C[r] for r in on_chip[ch]]) for ch in chips if ch != home}
+    pairs = [(j, d) for j in range(N) for d in chips if d != chip_of[j] and d != direct[j]]
+    pairs.sort(key=lambda p: (p[1] in reach[p[0]], p[0], not topo.mates(chip_of[p[0]], p[1]), p[1]))
+    relay = {}
+    wroute = {}
+
+    def route_x(j, d):
+        got = []
+        for r in on_chip[d]:
+            c = pick(C[j], [C[r]], reuse=[k for k in got if topo.chip(k) == d])
+            got.append(c)
+            relay[(j, r)] = c
+
+    for (j, d) in pairs:
+        if d not in reach[j]:
+            route_x(j, d)
+    for q, o in enumerate(owners):
+        for d in chips:
+            if d != home and d not in reach[o]:
+                for r in on_chip[d]:
+                    wroute.setdefault(pick(C[o], [C[r]]), []).append((q, [r]))
+    for (j, d) in pairs:
+        if d in reach[j]:
+            route_x(j, d)
+    wdst = {}
+    for q, o in enumerate(owners):
+        for d in chips:
+            if d != home and d in reach[o]:
+                c = pick(C[o], [C[r] for r in on_chip[d]], dst_first=True, reuse=wdst.get(d, []))
+                wdst.setdefault(d, []).append(c)
+                wroute.setdefault(c, []).append((q, list(on_chip[d])))
+
+    score = {}
+    for j in range(N):
+        for r in range(N):
+            if r == j:
+                score[(r, j)] = 0
+            elif (j, r) in relay:
+                score[(r, j)] = 2 if chip_of[r] in reach[j] else 3
+            else:
+                score[(r, j)] = 1
 
     for j in range(N):
         src = C[j]
-        near, direct, blocked, relay = route[j]
+        mate = [p for p in on_chip[chip_of[j]] if p != j]
+        onb = _bits(common(src, [C[p] for p in mate]))
         if j in owners:
             q = owners.index(j)
-            wc = (q * M, (q + 1) * M)
-            dl = [whelp[ch] for ch in sorted(whelp)] + [C[r] for r in on_chip[home] if r != j]
-            add(src, [("ldw", 16)], [("wcat", wc, [(d, "wcat", wc) for d in dl], "aw", common(src, dl))])
-        if blocked:
-            hs = sorted(blocked)
-            trs = []
-            for i, h in enumerate(hs):
-                b = _bits(topo.mask(src, relay[h]))
-                n = len(b) // len(hs)
-                trs.append(("xs", (h * H, (h + 1) * H), [(relay[h], "hl", None)], "ah", _mk(b[i * n:(i + 1) * n])))
-            add(src, [("ldx", 16)], trs)
-            for h in hs:
-                ds = [C[r] for r in blocked[h]]
-                add(relay[h], [("ah", None)],
-                    [("hl", None, [(d, "land%d" % j, None) for d in ds], "a%d" % j, common(relay[h], ds))])
-        trs = []
-        used = []
-        hs = sorted(direct)
-        for i, h in enumerate(hs):
-            ds = [C[r] for r in direct[h]]
-            b = _bits(common(src, ds))
-            n = len(b) // len(hs)
-            used += b
-            trs.append(("xs", (h * H, (h + 1) * H), [(d, "land%d" % j, None) for d in ds], "a%d" % j,
-                        _mk(b[i * n:(i + 1) * n])))
-        for r in near:
-            b = [e for e in _bits(topo.mask(src, C[r])) if e not in used]
-            h = half[r]
-            trs.append(("xs", (h * H, (h + 1) * H), [(C[r], "land%d" % j, None)], "a%d" % j, _mk(b)))
-        add(src, [("ldx", 16)], trs)
-    for ch in sorted(whelp):
-        ds = [C[r] for r in on_chip[ch]]
-        add(whelp[ch], [("aw", None)], [("wcat", None, [(d, "wcat", None) for d in ds], "aw", common(whelp[ch], ds))])
+            dl = sorted(c for c in wroute if any(qq == q for (qq, _r) in wroute[c]))
+            add(src, [("ldw", 16)], [("wd", None, [(c, "wh", ("s", q)) for c in dl], "aw", common(src, dl))])
+        feeds = {}
+        for r in range(N):
+            if (j, r) in relay and relay[(j, r)] not in feeds.setdefault(half[r], []):
+                feeds[half[r]].append(relay[(j, r)])
+        hs = sorted(feeds)
+        bl = {h: _bits(common(src, feeds[h])) for h in hs}
+        use = {}
+        if len(hs) == 1:
+            use[hs[0]] = bl[hs[0]]
+        elif bl[hs[0]] == bl[hs[1]]:
+            n = len(bl[hs[0]]) // 2
+            use[hs[0]], use[hs[1]] = bl[hs[0]][:n], bl[hs[1]][n:]
+        else:
+            a, b = sorted(hs, key=lambda h: len(bl[h]))
+            use[a] = bl[a]
+            use[b] = [e for e in bl[b] if e not in bl[a]]
+        add(src, [("ldx", 32)],
+            [("xd", ("s", h), [(c, "hd", ("s", h)) for c in feeds[h]], "ah", _mk(use[h])) for h in hs])
+        trs, used = [], []
+        if direct[j] is not None:
+            rs = on_chip[direct[j]]
+            b = _bits(common(src, [C[r] for r in rs]))
+            n = len(b) // len(rs)
+            used = b
+            for i, r in enumerate(rs):
+                trs.append(("xd", ("s", half[r]), [(C[r], "land%d" % j, None)], "a%d" % j, _mk(b[i * n:(i + 1) * n])))
+        for p in mate:
+            trs.append(("xd", ("s", half[p]), [(C[p], "land%d" % j, None)], "a%d" % j,
+                        _mk([e for e in onb if e not in used])))
+        add(src, [], trs)
+        if j in owners:
+            q = owners.index(j)
+            dl = [C[r] for r in on_chip[home] if r != j]
+            add(src, [], [("wd", None, [(d, "wcat", ("c", q * M, (q + 1) * M)) for d in dl], "aw", common(src, dl))])
+
+    hx = {}
+    for (j, r) in sorted(relay):
+        hx.setdefault(relay[(j, r)], []).append((j, r))
+    for c in sorted(hx):
+        b = _bits(common(c, [C[r] for (_j, r) in hx[c]]))
+        n = len(b) // len(hx[c])
+        add(c, [("ah", None)], [("hd", ("s", half[r]), [(C[r], "land%d" % j, None)], "a%d" % j,
+                                 _mk(b[i * n:(i + 1) * n])) for i, (j, r) in enumerate(hx[c])])
+    for c in sorted(wroute):
+        b = _bits(common(c, [C[r] for (_q, rs) in wroute[c] for r in rs]))
+        n = len(b) // len(wroute[c])
+        add(c, [("aw", None)], [("wh", ("s", q), [(C[r], "wcat", ("c", q * M, (q + 1) * M)) for r in rs], "aw",
+                                 _mk(b[i * n:(i + 1) * n])) for i, (q, rs) in enumerate(wroute[c])])
     for j in range(N):
-        for r in route[j][0]:
-            add(C[j], [("vy", 1)], [("yh", None, [(C[r], "yo", None)], "ay", topo.mask(C[j], C[r]))])
-    return {"calls": calls, "expect": expect, "cls": cls, "half": half, "owners": owners, "groups": G}
+        for p in on_chip[chip_of[j]]:
+            if p != j:
+                add(C[j], [("vy0", 1), ("vy1", 1)], [("yh", None, [(C[p], "yo", None)], "ay", topo.mask(C[j], C[p]))])
+    return {"calls": calls, "expect": expect, "score": score, "half": half, "owners": owners, "groups": G}
 
 
 def rank_program(g, core, T, topo):
@@ -149,8 +217,13 @@ def rank_program(g, core, T, topo):
     S = T.sem
     rank = T.rank_of(core)
 
-    def ap(name, cols):
-        return T[name][:] if cols is None else T[name][:, cols[0]:cols[1]]
+    def ap(name, part):
+        t = T[name]
+        if part is None:
+            return t[:]
+        if part[0] == "s":
+            return t[part[1]]
+        return t[:, part[1]:part[2]]
 
     def issue():
         sent = 0
@@ -176,60 +249,96 @@ def rank_program(g, core, T, topo):
     h = P["half"][rank]
     own = (h * H, (h + 1) * H)
     oth = ((1 - h) * H, (2 - h) * H)
-    V, PE = g.vector, g.tensor
+    V, PE, ACT = g.vector, g.tensor, g.scalar
+    owner = rank in P["owners"]
 
-    if rank in P["owners"]:
+    if owner:
+        g.sync.dma_start(T.wd[:], T.w[:]).then_inc(S.ldw, 16)
+    g.sync.dma_start(T.xd[0], T.x[:, 0:H]).then_inc(S.ldx, 16)
+    g.scalar.dma_start(T.xd[1], T.x[:, H:F]).then_inc(S.ldx, 16)
+    g.sync.dma_start(T.xo[:], T.x[:, own[0]:own[1]]).then_inc(S.ldo, 16)
+    if owner:
         q = P["owners"].index(rank)
-        g.scalar.dma_start(T.wcat[:, q * M:(q + 1) * M], T.w[:]).then_inc(S.ldw, 16)
-    g.sync.dma_start(T.xs[:], T.x[:]).then_inc(S.ldx, 16)
-    V.memset(T.zero[:], 0.0).then_inc(S.zs, 1)
+        g.scalar.dma_start(T.wcat[:, q * M:(q + 1) * M], T.w[:]).then_inc(S.ldc, 16)
+
+    V.memset(T.ones[:], 1.0).then_inc(S.zs, 1)
+    g.wait_ge(S.zs, 1)
+    g.affine_select(out=T.ident[:], in_=T.ones[:], pattern=[[-1, 128]], compare_op=AluOpType.is_equal, fill=0.0,
+                    base=0, channel_multiplier=1).then_inc(S.idn, 1)
 
     def piece(j):
         if j == rank:
-            return ap("xs", own), ("ldx", 16)
-        return T["land%d" % j][:], ("a%d" % j, expect[(core, "a%d" % j)])
+            return T.xo, ("ldo", 16)
+        return T["land%d" % j], ("a%d" % j, expect[(core, "a%d" % j)])
 
-    cls = P["cls"]
-    order = {}
-    for q, mem in enumerate(P["groups"]):
-        order[q] = sorted(mem, key=lambda j: cls[(rank, j)])
-    gs = sorted(order, key=lambda q: cls[(rank, order[q][-1])])
-    ops = []
-    for q in gs:
-        ops.append((cls[(rank, order[q][1])], "A", q))
-        ops.append((cls[(rank, order[q][2])], "B", q))
-        ops.append((cls[(rank, order[q][2])], "T", q))
-    ops.sort(key=lambda o: o[0])
-    for (_k, kind, q) in ops:
-        pa, pb = T["pa%d" % q][:, 0:H], T["pb%d" % q][:, 0:H]
-        if kind == "A":
-            (a0, w0), (a1, w1) = piece(order[q][0]), piece(order[q][1])
-            V.wait_ge(S[w0[0]], w0[1])
-            V.wait_ge(S[w1[0]], w1[1])
-            V.tensor_tensor(out=pa, in0=a0, in1=a1, op=AluOpType.add).then_inc(S["va%d" % q], 1)
-        elif kind == "B":
-            a2, w2 = piece(order[q][2])
-            V.wait_ge(S[w2[0]], w2[1])
-            V.wait_ge(S["va%d" % q], 1)
-            V.tensor_tensor(out=pb, in0=pa, in1=a2, op=AluOpType.add).then_inc(S["vb%d" % q], 1)
-        else:
-            V.wait_ge(S.zs, 1)
-            V.wait_ge(S["vb%d" % q], 1)
-            V.tensor_tensor(out=T["t%d" % q][:], in0=pb, in1=T.zero[:], op=AluOpType.max).then_inc(S["vt%d" % q], 1)
+    sc = P["score"]
+    order = {q: sorted(mem, key=lambda j: (sc[(rank, j)], j)) for q, mem in enumerate(P["groups"])}
+    ga, gb = sorted(order, key=lambda q: (sc[(rank, order[q][-1])], -q))
+    jl = order[gb][-1]
+    on_pe = {ga: list(order[ga]), gb: list(order[gb][:-1])}
 
-    if rank in P["owners"]:
-        PE.wait_ge(S.ldw, 16)
+    def cols(c):
+        return slice(c * CW, (c + 1) * CW)
+
+    def sum_in(q, j):
+        buf, w = piece(j)
+        PE.wait_ge(S[w[0]], w[1])
+        for c in range(NCH):
+            mm = PE.matmul(out=T["s%d%d" % (q, c)][:, 0:CW], lhsT=T.ident[:], rhs=buf[:, cols(c)],
+                           start=(j == on_pe[q][0]), stop=(j == on_pe[q][-1]))
+            if j == on_pe[q][-1]:
+                mm.then_inc(S["ps%d%d" % (q, c)], 1)
+
+    def w_mm(q, c, first):
+        PE.wait_ge(S["vt%d%d" % (q, c)], 1)
+        mm = PE.matmul(out=T["py%d" % c][:, 0:CW], lhsT=T.wcat[:, q * M:(q + 1) * M], rhs=T["t%d" % q][:, cols(c)],
+                       start=first, stop=not first)
+        if not first:
+            mm.then_inc(S["pm%d" % c], 1)
+
+    PE.wait_ge(S.idn, 1)
+    for q in (ga, gb):
+        for j in on_pe[q]:
+            if sc[(rank, j)] <= 1:
+                sum_in(q, j)
+    for j in on_pe[ga]:
+        if sc[(rank, j)] > 1:
+            sum_in(ga, j)
+    if owner:
+        PE.wait_ge(S.ldc, 16)
     PE.wait_ge(S.aw, expect[(core, "aw")])
-    for i, q in enumerate(gs):
-        PE.wait_ge(S["vt%d" % q], 1)
-        mm = PE.matmul(out=T.py[:, 0:H], lhsT=T.wcat[:, q * M:(q + 1) * M], rhs=T["t%d" % q][:],
-                       start=(i == 0), stop=(i == len(gs) - 1))
-        if i == len(gs) - 1:
-            mm.then_inc(S.pm, 1)
-    V.wait_ge(S.pm, 1)
-    V.tensor_copy(out=T.yh[:], in_=T.py[:, 0:H]).then_inc(S.vy, 1)
+    w_mm(ga, 0, True)
+    w_mm(ga, 1, True)
+    for j in on_pe[gb]:
+        if sc[(rank, j)] > 1:
+            sum_in(gb, j)
+    w_mm(gb, 1, False)
+    w_mm(gb, 0, False)
 
-    g.sync.wait_ge(S.vy, 1)
+    lbuf, lw = piece(jl)
+    V.wait_ge(S[lw[0]], lw[1])
+    for c in (1, 0):
+        sb = T["s%d%d" % (gb, c)][:, 0:CW]
+        V.wait_ge(S["ps%d%d" % (gb, c)], 1)
+        V.tensor_tensor(out=sb, in0=sb, in1=lbuf[:, cols(c)], op=AluOpType.add).then_inc(S["vs%d" % c], 1)
+    V.wait_ge(S.vs0, 1)
+    V.tensor_scalar(out=T["t%d" % gb][:, cols(0)], in0=T["s%d0" % gb][:, 0:CW], scalar1=0.0, scalar2=None,
+                    op0=AluOpType.max).then_inc(S["vt%d0" % gb], 1)
+    V.wait_ge(S.pm0, 1)
+    V.tensor_copy(out=T.yh[:, cols(0)], in_=T.py0[:, 0:CW]).then_inc(S.vy0, 1)
+
+    for c in range(NCH):
+        ACT.wait_ge(S["ps%d%d" % (ga, c)], 1)
+        ACT.activation(out=T["t%d" % ga][:, cols(c)], in_=T["s%d%d" % (ga, c)][:, 0:CW],
+                       func=ActivationFunctionType.Relu).then_inc(S["vt%d%d" % (ga, c)], 1)
+    ACT.wait_ge(S.vs1, 1)
+    ACT.activation(out=T["t%d" % gb][:, cols(1)], in_=T["s%d1" % gb][:, 0:CW],
+                   func=ActivationFunctionType.Relu).then_inc(S["vt%d1" % gb], 1)
+    ACT.wait_ge(S.pm1, 1)
+    ACT.activation(out=T.yh[:, cols(1)], in_=T.py1[:, 0:CW], func=ActivationFunctionType.Copy).then_inc(S.vy1, 1)
+
+    g.sync.wait_ge(S.vy0, 1)
+    g.sync.wait_ge(S.vy1, 1)
     g.sync.dma_start(T.y[:, own[0]:own[1]], T.yh[:]).then_inc(S.st1, 16)
     g.scalar.wait_ge(S.ay, expect[(core, "ay")])
     g.scalar.dma_start(T.y[:, oth[0]:oth[1]], T.yo[:]).then_inc(S.st2, 16)

from concourse.bass import DstId, RemoteDMATransfer
from concourse.mybir import AluOpType, ActivationFunctionType

F = 512
H = 256
M = 128
NCH = 2
CW = H // NCH

SCRATCH = {
    "xd": ("dram", [2, 128, H], "bfloat16"),
    "hd": ("dram", [2, 128, H], "bfloat16"),
    "wd": ("dram", [128, M], "bfloat16"),
    "wh": ("dram", [2, 128, M], "bfloat16"),
    "xo": ("sbuf", [128, H], "bfloat16"),
    "wcat": ("sbuf", [128, 2 * M], "bfloat16"),
    "land0": ("sbuf", [128, H], "bfloat16"),
    "land1": ("sbuf", [128, H], "bfloat16"),
    "land2": ("sbuf", [128, H], "bfloat16"),
    "land3": ("sbuf", [128, H], "bfloat16"),
    "land4": ("sbuf", [128, H], "bfloat16"),
    "land5": ("sbuf", [128, H], "bfloat16"),
    "ones": ("sbuf", [128, 128], "bfloat16"),
    "ident": ("sbuf", [128, 128], "bfloat16"),
    "t0": ("sbuf", [128, H], "bfloat16"),
    "t1": ("sbuf", [128, H], "bfloat16"),
    "yh": ("sbuf", [128, H], "bfloat16"),
    "yo": ("sbuf", [128, H], "bfloat16"),
    "s00": ("psum", [128, 512], "float32"),
    "s01": ("psum", [128, 512], "float32"),
    "s10": ("psum", [128, 512], "float32"),
    "s11": ("psum", [128, 512], "float32"),
    "py0": ("psum", [128, 512], "float32"),
    "py1": ("psum", [128, 512], "float32"),
}
SEMAPHORES = ["ldx", "ldw", "ldo", "ldc", "zs", "idn", "ah", "aw", "a0", "a1", "a2", "a3", "a4", "a5",
              "ps00", "ps01", "ps10", "ps11", "vs0", "vs1", "vt00", "vt01", "vt10", "vt11", "pm0", "pm1",
              "vy0", "vy1", "ay", "st1", "st2", "ls"]


def _bits(mask):
    return [i for i in range(mask.bit_length()) if (mask >> i) & 1]


def _mk(bits):
    m = 0
    for b in bits:
        m |= 1 << b
    return m


def _plan(T, topo):
    C = list(T.cores)
    G = T.tables["GROUPS"]
    N = len(C)
    chip_of = [topo.chip(c) for c in C]
    chips = sorted(set(chip_of))
    on_chip = {ch: [r for r in range(N) if chip_of[r] == ch] for ch in chips}
    half = {}
    for ch in chips:
        for i, r in enumerate(on_chip[ch]):
            half[r] = i
    every = range(topo.CHIPS * topo.CORES_PER_CHIP)
    spare = [c for c in every if c not in C and
             (topo.chip(c) in chips or any(topo.mates(topo.chip(c), ch) for ch in chips))]

    def pick(src, dsts, dst_first=False, reuse=()):
        def ok(c):
            return topo.may_write(src, c) and all(topo.may_write(c, d) for d in dsts)

        def key(c):
            if topo.chip(c) == topo.chip(src):
                return (1 if dst_first else 0, topo.die(c) == topo.die(src), c)
            if topo.chip(c) == topo.chip(dsts[0]):
                return (0 if dst_first else 1, topo.die(c) != topo.die(dsts[0]), c)
            return (2, topo.die(c) == topo.die(src), c)
        c = sorted([c for c in list(spare) + list(reuse) if ok(c)], key=key)[0]
        if c in spare:
            spare.remove(c)
        return c

    calls, expect = {}, {}

    def add(core, waits, trs):
        calls.setdefault(core, []).append((waits, trs))
        for (_sn, _sc, dl, sem, mask) in trs:
            for (dc, _dn, _dcs) in dl:
                expect[(dc, sem)] = expect.get((dc, sem), 0) + len(_bits(mask))

    def common(src, dsts):
        m = topo.mask(src, dsts[0])
        for d in dsts[1:]:
            m &= topo.mask(src, d)
        return m

    reach = {j: [d for d in chips if d != chip_of[j] and all(topo.may_write(C[j], C[r]) for r in on_chip[d])]
             for j in range(N)}
    direct = {}
    for j in sorted(range(N), key=lambda j: (len(reach[j]), j)):
        if not reach[j]:
            direct[j] = None
            continue
        taken = [direct.get(p) for p in on_chip[chip_of[j]] if p != j]
        direct[j] = sorted(reach[j], key=lambda d: (d in taken, not topo.mates(chip_of[j], d), d))[0]

    owners = [m[0] for m in G]
    home = chip_of[owners[0]]
    pairs = [(j, d) for j in range(N) for d in chips if d != chip_of[j] and d != direct[j]]
    pairs.sort(key=lambda p: (p[1] in reach[p[0]], p[0], not topo.mates(chip_of[p[0]], p[1]), p[1]))
    relay = {}
    wroute = {}

    def route_x(j, d):
        got = []
        for r in on_chip[d]:
            c = pick(C[j], [C[r]], reuse=[k for k in got if topo.chip(k) == d])
            got.append(c)
            relay[(j, r)] = c

    for (j, d) in pairs:
        if d not in reach[j]:
            route_x(j, d)
    for q, o in enumerate(owners):
        for d in chips:
            if d != home and d not in reach[o]:
                for r in on_chip[d]:
                    wroute.setdefault(pick(C[o], [C[r]]), []).append((q, [r]))
    for (j, d) in pairs:
        if d in reach[j]:
            route_x(j, d)
    wdst = {}
    for q, o in enumerate(owners):
        for d in chips:
            if d != home and d in reach[o]:
                c = pick(C[o], [C[r] for r in on_chip[d]], dst_first=True, reuse=wdst.get(d, []))
                wdst.setdefault(d, []).append(c)
                wroute.setdefault(c, []).append((q, list(on_chip[d])))

    score = {}
    for j in range(N):
        for r in range(N):
            if r == j:
                score[(r, j)] = 0
            elif (j, r) in relay:
                score[(r, j)] = 2 if chip_of[r] in reach[j] else 3
            else:
                score[(r, j)] = 1

    for j in range(N):
        src = C[j]
        mate = [p for p in on_chip[chip_of[j]] if p != j]
        onb = _bits(common(src, [C[p] for p in mate]))
        if j in owners:
            q = owners.index(j)
            dl = sorted(c for c in wroute if any(qq == q for (qq, _r) in wroute[c]))
            add(src, [("ldw", 16)], [("wd", None, [(c, "wh", ("s", q)) for c in dl], "aw", common(src, dl))])
        feeds = {}
        for r in range(N):
            if (j, r) in relay and relay[(j, r)] not in feeds.setdefault(half[r], []):
                feeds[half[r]].append(relay[(j, r)])
        hs = sorted(feeds)
        bl = {h: _bits(common(src, feeds[h])) for h in hs}
        use = {}
        if len(hs) == 1:
            use[hs[0]] = bl[hs[0]]
        elif bl[hs[0]] == bl[hs[1]]:
            n = len(bl[hs[0]]) // 2
            use[hs[0]], use[hs[1]] = bl[hs[0]][:n], bl[hs[1]][n:]
        else:
            a, b = sorted(hs, key=lambda h: len(bl[h]))
            use[a] = bl[a]
            use[b] = [e for e in bl[b] if e not in bl[a]]
        add(src, [("ldx", 32)],
            [("xd", ("s", h), [(c, "hd", ("s", h)) for c in feeds[h]], "ah", _mk(use[h])) for h in hs])
        trs, used = [], []
        if direct[j] is not None:
            rs = on_chip[direct[j]]
            b = _bits(common(src, [C[r] for r in rs]))
            n = len(b) // len(rs)
            used = b
            for i, r in enumerate(rs):
                trs.append(("xd", ("s", half[r]), [(C[r], "land%d" % j, None)], "a%d" % j, _mk(b[i * n:(i + 1) * n])))
        for p in mate:
            trs.append(("xd", ("s", half[p]), [(C[p], "land%d" % j, None)], "a%d" % j,
                        _mk([e for e in onb if e not in used])))
        add(src, [], trs)
        if j in owners:
            q = owners.index(j)
            dl = [C[r] for r in on_chip[home] if r != j]
            add(src, [], [("wd", None, [(d, "wcat", ("c", q * M, (q + 1) * M)) for d in dl], "aw", common(src, dl))])

    hx = {}
    for (j, r) in sorted(relay):
        hx.setdefault(relay[(j, r)], []).append((j, r))
    for c in sorted(hx):
        b = _bits(common(c, [C[r] for (_j, r) in hx[c]]))
        n = len(b) // len(hx[c])
        add(c, [("ah", None)], [("hd", ("s", half[r]), [(C[r], "land%d" % j, None)], "a%d" % j,
                                 _mk(b[i * n:(i + 1) * n])) for i, (j, r) in enumerate(hx[c])])
    for c in sorted(wroute):
        b = _bits(common(c, [C[r] for (_q, rs) in wroute[c] for r in rs]))
        n = len(b) // len(wroute[c])
        add(c, [("aw", None)], [("wh", ("s", q), [(C[r], "wcat", ("c", q * M, (q + 1) * M)) for r in rs], "aw",
                                 _mk(b[i * n:(i + 1) * n])) for i, (q, rs) in enumerate(wroute[c])])
    for j in range(N):
        for p in on_chip[chip_of[j]]:
            if p != j:
                add(C[j], [("vy0", 1), ("vy1", 1)], [("yh", None, [(C[p], "yo", None)], "ay", topo.mask(C[j], C[p]))])
    return {"calls": calls, "expect": expect, "score": score, "half": half, "owners": owners, "groups": G}


def rank_program(g, core, T, topo):
    P = _plan(T, topo)
    calls, expect = P["calls"], P["expect"]
    if core not in calls:
        return
    S = T.sem
    rank = T.rank_of(core)

    def ap(name, part):
        t = T[name]
        if part is None:
            return t[:]
        if part[0] == "s":
            return t[part[1]]
        return t[:, part[1]:part[2]]

    def issue():
        sent = 0
        for waits, trs in calls[core]:
            for s, v in waits:
                g.wait_ge(S[s], expect[(core, s)] if v is None else v)
            lst = []
            for (sn, sc, dl, sem, mask) in trs:
                ids = []
                for (dc, _dn, _dcs) in dl:
                    rid, pid, _se = topo.addr(dc)
                    ids.append(DstId(rid=rid, pnc=pid))
                lst.append(RemoteDMATransfer(dst_ids=ids, dma_engine_mask=mask, remote_sem=S[sem],
                                             srcs=[ap(sn, sc)], dsts=[ap(dn, dcs) for (_dc, dn, dcs) in dl], alu_op=0))
                sent += len(_bits(mask))
            g.remote_dma_fused(lst, local_sem=S.ls)
        return sent

    if rank is None:
        g.wait_ge(S.ls, issue())
        return

    h = P["half"][rank]
    own = (h * H, (h + 1) * H)
    oth = ((1 - h) * H, (2 - h) * H)
    V, PE, ACT = g.vector, g.tensor, g.scalar
    owner = rank in P["owners"]

    if owner:
        g.sync.dma_start(T.wd[:], T.w[:]).then_inc(S.ldw, 16)
    g.sync.dma_start(T.xd[0], T.x[:, 0:H]).then_inc(S.ldx, 16)
    g.scalar.dma_start(T.xd[1], T.x[:, H:F]).then_inc(S.ldx, 16)
    g.sync.dma_start(T.xo[:], T.x[:, own[0]:own[1]]).then_inc(S.ldo, 16)
    if owner:
        q = P["owners"].index(rank)
        g.scalar.dma_start(T.wcat[:, q * M:(q + 1) * M], T.w[:]).then_inc(S.ldc, 16)

    V.memset(T.ones[:], 1.0).then_inc(S.zs, 1)
    g.wait_ge(S.zs, 1)
    g.affine_select(out=T.ident[:], in_=T.ones[:], pattern=[[-1, 128]], compare_op=AluOpType.is_equal, fill=0.0,
                    base=0, channel_multiplier=1).then_inc(S.idn, 1)

    def piece(j):
        if j == rank:
            return T.xo, ("ldo", 16)
        return T["land%d" % j], ("a%d" % j, expect[(core, "a%d" % j)])

    sc = P["score"]
    order = {q: sorted(mem, key=lambda j: (sc[(rank, j)], j)) for q, mem in enumerate(P["groups"])}
    ga, gb = sorted(order, key=lambda q: (sc[(rank, order[q][-1])], -q))
    jl = order[gb][-1]
    on_pe = {ga: list(order[ga]), gb: list(order[gb][:-1])}

    def cols(c):
        return slice(c * CW, (c + 1) * CW)

    def sum_in(q, j):
        buf, w = piece(j)
        PE.wait_ge(S[w[0]], w[1])
        for c in range(NCH):
            mm = PE.matmul(out=T["s%d%d" % (q, c)][:, 0:CW], lhsT=T.ident[:], rhs=buf[:, cols(c)],
                           start=(j == on_pe[q][0]), stop=(j == on_pe[q][-1]))
            if j == on_pe[q][-1]:
                mm.then_inc(S["ps%d%d" % (q, c)], 1)

    def w_mm(q, c, first):
        PE.wait_ge(S["vt%d%d" % (q, c)], 1)
        mm = PE.matmul(out=T["py%d" % c][:, 0:CW], lhsT=T.wcat[:, q * M:(q + 1) * M], rhs=T["t%d" % q][:, cols(c)],
                       start=first, stop=not first)
        if not first:
            mm.then_inc(S["pm%d" % c], 1)

    PE.wait_ge(S.idn, 1)
    for q in (ga, gb):
        for j in on_pe[q]:
            if sc[(rank, j)] <= 1:
                sum_in(q, j)
    for j in on_pe[ga]:
        if sc[(rank, j)] > 1:
            sum_in(ga, j)
    if owner:
        PE.wait_ge(S.ldc, 16)
    PE.wait_ge(S.aw, expect[(core, "aw")])
    w_mm(ga, 0, True)
    w_mm(ga, 1, True)
    for j in on_pe[gb]:
        if sc[(rank, j)] > 1:
            sum_in(gb, j)
    w_mm(gb, 1, False)
    w_mm(gb, 0, False)

    lbuf, lw = piece(jl)
    V.wait_ge(S[lw[0]], lw[1])
    for c in (1, 0):
        sb = T["s%d%d" % (gb, c)][:, 0:CW]
        V.wait_ge(S["ps%d%d" % (gb, c)], 1)
        V.tensor_tensor(out=sb, in0=sb, in1=lbuf[:, cols(c)], op=AluOpType.add).then_inc(S["vs%d" % c], 1)
    V.wait_ge(S.vs0, 1)
    V.tensor_scalar(out=T["t%d" % gb][:, cols(0)], in0=T["s%d0" % gb][:, 0:CW], scalar1=0.0, scalar2=None,
                    op0=AluOpType.max).then_inc(S["vt%d0" % gb], 1)
    V.wait_ge(S.pm0, 1)
    V.tensor_copy(out=T.yh[:, cols(0)], in_=T.py0[:, 0:CW]).then_inc(S.vy0, 1)

    for c in range(NCH):
        ACT.wait_ge(S["ps%d%d" % (ga, c)], 1)
        ACT.activation(out=T["t%d" % ga][:, cols(c)], in_=T["s%d%d" % (ga, c)][:, 0:CW],
                       func=ActivationFunctionType.Relu).then_inc(S["vt%d%d" % (ga, c)], 1)
    ACT.wait_ge(S.vs1, 1)
    ACT.activation(out=T["t%d" % gb][:, cols(1)], in_=T["s%d1" % gb][:, 0:CW],
                   func=ActivationFunctionType.Relu).then_inc(S["vt%d1" % gb], 1)
    ACT.wait_ge(S.pm1, 1)
    ACT.activation(out=T.yh[:, cols(1)], in_=T.py1[:, 0:CW], func=ActivationFunctionType.Copy).then_inc(S.vy1, 1)

    g.sync.wait_ge(S.vy0, 1)
    g.sync.wait_ge(S.vy1, 1)
    g.sync.dma_start(T.y[:, own[0]:own[1]], T.yh[:]).then_inc(S.st1, 16)
    g.scalar.wait_ge(S.ay, expect[(core, "ay")])
    g.scalar.dma_start(T.y[:, oth[0]:oth[1]], T.yo[:]).then_inc(S.st2, 16)

    g.wait_ge(S.ls, issue())
    g.wait_ge(S.st1, 16)
    g.wait_ge(S.st2, 16)
